import numpy as np
import ml_dtypes


def mxq(x, axis, fmt="e4m3"):
    dtype, down = {"e4m3": (ml_dtypes.float8_e4m3fn, 7), "e5m2": (ml_dtypes.float8_e5m2, 14)}[fmt]
    v = np.moveaxis(np.asarray(x, np.float32).astype(ml_dtypes.bfloat16).astype(np.float64), axis, -1)
    blocks = v.reshape(v.shape[:-1] + (-1, 32))
    amax = np.abs(blocks).max(-1, keepdims=True)
    byte = np.maximum(np.where(amax > 0, np.frexp(amax)[1] - 1 + 127, 0) - down, 1)
    scale = np.exp2(byte - 127.0)
    codes = (blocks / scale).astype(np.float32).astype(dtype).astype(np.float64)
    return np.moveaxis((codes * scale).reshape(v.shape), -1, axis)


WIDE = False


def mx_kscale(k):
    if not WIDE:
        return np.ones(k)
    levels = np.array([10, -10, 5, -5, 0])
    if k % 512:
        return np.exp2(np.random.permutation(np.resize(levels, k // 32))).repeat(32)
    a = np.empty((k // 512, 16))
    for p in range(k // 512):
        a[p, :8] = np.random.permutation(np.resize(levels, 8))
        for g in range(8):
            far = levels[np.abs(levels - a[p, g]) >= 10]
            a[p, g + 8] = far[np.random.randint(len(far))]
    return np.exp2(a.ravel()).repeat(32)


def f64(x):
    return np.asarray(x).astype(np.float64)


def striped(idx):
    return np.tile(idx.reshape(-1, 16).T, (8, 1)).astype(np.uint16)


def unstriped(offs):
    return offs[:16].T.reshape(-1).astype(np.int64)


def pack_weight(w):
    k, n = w.shape
    w = f64(np.asarray(w, np.float32).astype(ml_dtypes.bfloat16)).reshape(k // 32, 32, n)
    amax = np.abs(w).max(1)
    byte = np.clip(np.where(amax > 0, np.frexp(amax)[1] - 1 + 127 - 7, 1), 1, 254)
    scaled = (w * np.exp2(127.0 - byte)[:, None, :]).reshape(k, n).astype(np.float32)
    words = np.ascontiguousarray(scaled.reshape(k // 512, 128, 4, n).transpose(0, 1, 3, 2)).astype(ml_dtypes.float8_e4m3fn).view(np.uint8)
    return words, np.ascontiguousarray(byte.astype(np.uint8).reshape(k // 512, 16, n))


def unpack_weight(words, scales):
    g, p, n, _ = words.shape
    vals = np.ascontiguousarray(words).view(ml_dtypes.float8_e4m3fn).astype(np.float64) * np.repeat(np.exp2(scales.astype(np.float64) - 127.0), 8, axis=1)[..., None]
    return vals.transpose(0, 1, 3, 2).reshape(g * 512, n)


K, T, S, N, H, W = 512, 2048, 512, 512, 512, 2048


def setup_inputs():
    n = np.random.standard_normal
    s = mx_kscale(K)[:, None]
    u = mx_kscale(S)
    packed_xT = pack_weight(n((K, T)) * s)
    return {
        "x_words": packed_xT[0],
        "x_scales": packed_xT[1],
        "wa": (n((K, H)) / np.sqrt(K) / s).astype(np.float32),
        "gt": (np.random.uniform(0.5, 1.5, (S, 1)) * u[:, None]).astype(np.float32),
        "w1": (n((S, N)) / np.sqrt(S) / u[:, None]).astype(np.float32),
        "tau": np.random.uniform(0.3, 0.9, (N, 1)).astype(np.float32),
        "offs": striped(np.random.permutation(T)[:S]),
        "n1": striped(np.random.permutation(H)),
        "n2": striped(np.random.permutation(H)),
        "n3": striped(np.random.permutation(H)),
        "n4": striped(np.random.randint(0, H, W)),
    }


def reference(x_words, x_scales, wa, gt, w1, tau, offs, n1, n2, n3, n4):
    xq = unpack_weight(x_words, x_scales)[:, unstriped(offs)]
    y = xq.T @ mxq(f64(wa), 0, "e4m3")
    z = f64(gt) * (0.75 * (y * y[:, unstriped(n1)] + y[:, unstriped(n2)] * y[:, unstriped(n3)]))
    h = mxq(f64(w1), 0, "e4m3").T @ mxq(z, 0, "e4m3")
    top = h.max(axis=1, keepdims=True)
    ea = np.exp(f64(tau) * (h[:, unstriped(n4)] - top))
    mx = ea.reshape(N, H, 4).max(axis=2)
    mn = ea.reshape(N, H, 4).min(axis=2)
    return 3.0 * (h * (mx - mn))

@@ -1,0 +1,250 @@
+from contextlib import ExitStack
+
+import concourse.mybir as mybir
+
+K, T, S, N, H, W = 512, 2048, 512, 512, 512, 2048
+FLOPS = 2 * K * S * H + 2 * S * N * H
+
+F32 = mybir.dt.float32
+BF16 = mybir.dt.bfloat16
+I32 = mybir.dt.int32
+U32 = mybir.dt.uint32
+U16 = mybir.dt.uint16
+U8 = mybir.dt.uint8
+FP8X4 = mybir.dt.float8_e4m3fn_x4
+ALU = mybir.AluOpType
+ACT = mybir.ActivationFunctionType
+
+P = 128
+PACK = 4
+LIST_ROWS = 16
+MEMBERS = 4
+Z_CHUNKS = ((0, 384), (384, 128))
+EXP_OFFSETS = 512
+
+
+def weave_views(woven, planes):
+    return (
+        woven.rearrange("p (c i) t -> p c t i", i=4),
+        planes.rearrange("p t (c i) -> p c t i", i=4),
+    )
+
+
+def entries(offsets, first, count):
+    return offsets[:, first // LIST_ROWS : (first + count) // LIST_ROWS]
+
+
+def tile_picked_tokdotegp_none_p_kernel(
+    tc, x_words, x_scales, wa, gt, w1, tau, offs, n1, n2, n3, n4, out
+):
+    nc = tc.nc
+    with ExitStack() as ctx:
+        lists = ctx.enter_context(tc.tile_pool(name="lists", bufs=1))
+        keep = ctx.enter_context(tc.tile_pool(name="keep", bufs=1))
+        psum = ctx.enter_context(tc.psum_pool(name="psum", bufs=1))
+
+        offs_sb = lists.tile([P, S // LIST_ROWS], U16, name="offs_sb")
+        n1_sb = lists.tile([P, H // LIST_ROWS], U16, name="n1_sb")
+        n2_sb = lists.tile([P, H // LIST_ROWS], U16, name="n2_sb")
+        n3_sb = lists.tile([P, H // LIST_ROWS], U16, name="n3_sb")
+        n4_sb = lists.tile([P, W // LIST_ROWS], U16, name="n4_sb")
+
+        wa_raw = keep.tile([P, PACK, H], F32, name="wa_raw")
+        w1_raw = keep.tile([P, PACK, N], F32, name="w1_raw")
+        xw = keep.tile([P, T], I32, name="xw")
+        xs = keep.tile([P, T], U8, name="xs")
+        gt_sb = keep.tile([P, PACK], F32, name="gt_sb")
+        tau_sb = keep.tile([P, N // P, 1], F32, name="tau_sb")
+
+        nc.vector.memset(xs[:].bitcast(I32), 0)
+        nc.sync.dma_start(wa_raw[:], wa.rearrange("(p j) n -> p j n", j=PACK))
+        nc.sync.dma_start(offs_sb[:], offs)
+        for q in range(4):
+            nc.scalar.dma_start(
+                xs[32 * q : 32 * q + 4, :].bitcast(I32), x_scales[0, 4 * q : 4 * q + 4, :].bitcast(I32)
+            )
+        nc.sync.dma_start(xw[:], x_words[0].rearrange("p n r -> p (n r)").bitcast(I32))
+        nc.sync.dma_start(n3_sb[:], n3)
+        nc.sync.dma_start(n1_sb[:], n1)
+        nc.sync.dma_start(n2_sb[:], n2)
+        nc.sync.dma_start(gt_sb[:], gt.rearrange("(p j) o -> p (j o)", j=PACK))
+        nc.sync.dma_start(w1_raw[:], w1.rearrange("(p j) n -> p j n", j=PACK))
+        nc.sync.dma_start(n4_sb[:], n4)
+        with nc.allow_non_contiguous_dma(reason="one rate for each partition and block of rows"):
+            nc.sync.dma_start(tau_sb[:], tau.rearrange("(b p) o -> p b o", p=P))
+
+        xs_pick = keep.tile([P, S], U8, name="xs_pick", align_bytes=64)
+        xw_pick = keep.tile([P, S], U32, name="xw_pick", align_bytes=64)
+        nc.vector.tensor_copy(xs_pick[:].rearrange("p (t m) -> p m t", t=PACK), xs[:].indirect(offs_sb[:]))
+
+        wa_codes = keep.tile([P, H], U32, name="wa_codes", align_bytes=64)
+        wa_scales = keep.tile([P, H], U8, name="wa_scales", align_bytes=64)
+        half = H // 2
+        wa_lo = keep.tile([P, half, PACK], BF16, name="wa_lo", align_bytes=64)
+        wa_hi = keep.tile([P, half, PACK], BF16, name="wa_hi", align_bytes=64)
+        dst, src = weave_views(wa_lo[:], wa_raw[:, :, 0:half])
+        nc.vector.tensor_copy(dst, src)
+        dst, src = weave_views(wa_hi[:], wa_raw[:, :, half:H])
+        nc.scalar.activation(dst, src, ACT.Copy)
+        for first, woven in ((0, wa_lo), (half, wa_hi)):
+            nc.vector.quantize_mx(
+                out=wa_codes[:, first : first + half].bitcast(FP8X4),
+                scales=wa_scales[:, first : first + half],
+                in_=woven[:].rearrange("p n t -> p (n t)"),
+            )
+        nc.vector.tensor_copy(
+            xw_pick[:].rearrange("p (t m) -> p m t", t=PACK), xw[:].bitcast(U32).indirect(offs_sb[:])
+        )
+        gain = keep.tile([P, PACK], F32, name="gain")
+        nc.vector.tensor_scalar(gain[:], gt_sb[:], 0.75, None, ALU.mult)
+
+        y = []
+        for t in range(PACK):
+            bank = psum.tile([P, H], F32, name="y_bank%d" % t)
+            nc.tensor.matmul_mx(
+                out=bank[:],
+                lhsT=xw_pick[:, t * P : (t + 1) * P].bitcast(FP8X4),
+                lhsT_scale=xs_pick[:, t * P : (t + 1) * P],
+                rhs=wa_codes[:].bitcast(FP8X4),
+                rhs_scale=wa_scales[:],
+                start=True,
+                stop=True,
+            )
+            y_t = keep.tile([P, H], F32, name="y%d" % t)
+            if t in (1, 2):
+                nc.vector.tensor_copy(y_t[:], bank[:])
+            else:
+                nc.scalar.activation(y_t[:], bank[:], ACT.Copy)
+            y.append(y_t)
+
+        h = [keep.tile([P, 2 * H], F32, name="h%d" % b) for b in range(N // P)]
+        z_codes = keep.tile([P, H], U32, name="z_codes", align_bytes=64)
+        z_scales = keep.tile([P, H], U8, name="z_scales", align_bytes=64)
+        w1_codes = [keep.tile([P, P], U32, name="w1_codes%d" % b, align_bytes=64) for b in range(N // P)]
+        w1_scales = [keep.tile([P, P], U8, name="w1_scales%d" % b, align_bytes=64) for b in range(N // P)]
+        w1_woven = [keep.tile([P, P, PACK], BF16, name="w1_woven%d" % b, align_bytes=64) for b in range(N // P)]
+
+        def round_w1(b):
+            dst, src = weave_views(w1_woven[b][:], w1_raw[:, :, b * P : (b + 1) * P])
+            nc.scalar.activation(dst, src, ACT.Copy)
+
+        def quantize_w1(b):
+            nc.vector.quantize_mx(
+                out=w1_codes[b][:].bitcast(FP8X4),
+                scales=w1_scales[b][:],
+                in_=w1_woven[b][:].rearrange("p n t -> p (n t)"),
+            )
+
+        chunks = []
+        for chunk, (first, width) in enumerate(Z_CHUNKS):
+            cols = slice(first, first + width)
+            z_planes = keep.tile([P, PACK, width], BF16, name="z_planes%d" % chunk, align_bytes=64)
+            z_woven = keep.tile([P, width, PACK], BF16, name="z_woven%d" % chunk, align_bytes=64)
+            pending = None
+            for t in range(PACK):
+                y3 = keep.tile([P, width], F32, name="y3_%d_%d" % (chunk, t))
+                y1 = keep.tile([P, width], F32, name="y1_%d_%d" % (chunk, t))
+                cross = keep.tile([P, width], F32, name="cross_%d_%d" % (chunk, t))
+                own = h[t][:, H + first : H + first + width]
+                nc.scalar.activation(y3[:], y[t][:].indirect(entries(n3_sb, first, width)), ACT.Copy)
+                nc.scalar.activation(y1[:], y[t][:].indirect(entries(n1_sb, first, width)), ACT.Copy)
+                nc.vector.tensor_tensor(cross[:], y[t][:].indirect(entries(n2_sb, first, width)), y3[:], ALU.mult)
+                if pending is not None:
+                    nc.vector.scalar_tensor_tensor(*pending, ALU.mult, ALU.add)
+                nc.vector.scalar_tensor_tensor(own, y1[:], gain[:, t : t + 1], y[t][:, cols], ALU.mult, ALU.mult)
+                pending = (z_planes[:, t, :], cross[:], gain[:, t : t + 1], own)
+            nc.vector.scalar_tensor_tensor(*pending, ALU.mult, ALU.add)
+            chunks.append((cols, z_planes, z_woven))
+        round_w1(0)
+        for chunk, (cols, z_planes, z_woven) in enumerate(chunks):
+            dst, src = weave_views(z_woven[:], z_planes[:])
+            if chunk == 0:
+                nc.scalar.copy(dst, src)
+            else:
+                nc.vector.tensor_copy(dst, src)
+        quantize_w1(0)
+        for cols, z_planes, z_woven in chunks:
+            nc.vector.quantize_mx(
+                out=z_codes[:, cols].bitcast(FP8X4),
+                scales=z_scales[:, cols],
+                in_=z_woven[:].rearrange("p n t -> p (n t)"),
+            )
+
+        scale_bias = []
+
+        def second_product(b):
+            bank = psum.tile([P, H], F32, name="h_bank%d" % b)
+            for first, width in ((0, 256), (256, 128), (384, 128)):
+                cols = slice(first, first + width)
+                nc.tensor.matmul_mx(
+                    out=bank[:, cols],
+                    lhsT=w1_codes[b][:].bitcast(FP8X4),
+                    lhsT_scale=w1_scales[b][:],
+                    rhs=z_codes[:, cols].bitcast(FP8X4),
+                    rhs_scale=z_scales[:, cols],
+                    start=True,
+                    stop=True,
+                )
+            top = keep.tile([P, 1], F32, name="top%d" % b)
+            bias = keep.tile([P, 1], F32, name="bias%d" % b)
+            nc.vector.tensor_scalar(h[b][:, 0:H], bank[:], 1.0, None, ALU.mult, ALU.max, accum_out=top[:])
+            nc.vector.tensor_scalar(bias[:], top[:], tau_sb[:, b, :], -1.0, ALU.mult, ALU.mult)
+            scale_bias.append((tau_sb[:, b, :], bias[:]))
+
+        second_product(0)
+        for b in range(1, N // P):
+            round_w1(b)
+            quantize_w1(b)
+            second_product(b)
+
+        pieces = []
+        for b in range(N // P):
+            widths = ((128, 128, 256), (256, 256), (256, 256), (256, 128, 128))[b]
+            first = 0
+            for width in widths:
+                pieces.append((b, first, width))
+                first = first + width
+
+        previous = None
+
+        def finish_sub(state):
+            b, first, width, mx, mn, spread = state
+            nc.vector.tensor_tensor(spread[:], mx[:], mn[:], ALU.subtract)
+
+        def finish_out(state):
+            b, first, width, mx, mn, spread = state
+            result = keep.tile([P, width], F32, name="result_%d_%d" % (b, first))
+            nc.vector.scalar_tensor_tensor(
+                result[:], spread[:], 3.0, h[b][:, first : first + width], ALU.mult, ALU.mult
+            )
+            nc.sync.dma_start(out[b * P : (b + 1) * P, first : first + width], result[:])
+
+        for b, first, width in pieces:
+            scale, bias = scale_bias[b]
+            name = "_%d_%d" % (b, first)
+            ea = keep.tile([P, width, MEMBERS], F32, name="ea" + name)
+            flat = ea[:].rearrange("p j t -> p (j t)")
+            for e0 in range(0, width * MEMBERS, EXP_OFFSETS):
+                nc.scalar.activation(
+                    flat[:, e0 : e0 + EXP_OFFSETS],
+                    h[b][:].indirect(entries(n4_sb, first * MEMBERS + e0, EXP_OFFSETS)),
+                    ACT.Exp,
+                    bias=bias,
+                    scale=scale,
+                )
+            upper = keep.tile([P, width, 2], F32, name="upper" + name)
+            lower = keep.tile([P, width, 2], F32, name="lower" + name)
+            mx = keep.tile([P, width], F32, name="mx" + name)
+            mn = keep.tile([P, width], F32, name="mn" + name)
+            spread = keep.tile([P, width], F32, name="spread" + name)
+            nc.vector.tensor_tensor(upper[:], ea[:, :, 0:2], ea[:, :, 2:4], ALU.max)
+            nc.vector.tensor_tensor(lower[:], ea[:, :, 0:2], ea[:, :, 2:4], ALU.min)
+            if previous is not None:
+                finish_sub(previous)
+            nc.vector.tensor_tensor(mx[:], upper[:, :, 0], upper[:, :, 1], ALU.max)
+            if previous is not None:
+                finish_out(previous)
+            nc.vector.tensor_tensor(mn[:], lower[:, :, 0], lower[:, :, 1], ALU.min)
+            previous = (b, first, width, mx, mn, spread)
+        finish_sub(previous)
+        finish_out(previous)

@@ -19,7 +19,13 @@ P = 128
 PACK = 4
 LIST_ROWS = 16
 MEMBERS = 4
-Z_CHUNKS = ((0, 384), (384, 128))
+Z_CHUNKS = ((0, 384, 'vector'), (384, 128, 'scalar'))
+YENG = 'svvsv'
+LAST = (256, 256)
+MID = False
+ORDER = 1
+FIRST = (128, 128, 256)
+QSPLIT = True
 EXP_OFFSETS = 512
 
 
@@ -49,26 +55,36 @@ def tile_picked_tokdotegp_none_p_kernel(
         n3_sb = lists.tile([P, H // LIST_ROWS], U16, name="n3_sb")
         n4_sb = lists.tile([P, W // LIST_ROWS], U16, name="n4_sb")
 
-        wa_raw = keep.tile([P, PACK, H], F32, name="wa_raw")
-        w1_raw = keep.tile([P, PACK, N], F32, name="w1_raw")
+        half = H // 2
+        wa_raw = [keep.tile([P, PACK, half], F32, name="wa_raw%d" % u) for u in range(2)]
+        w1_first = keep.tile([P, PACK, P], F32, name="w1_first")
+        w1_rest = keep.tile([P, PACK, N - P], F32, name="w1_rest")
         xw = keep.tile([P, T], I32, name="xw")
         xs = keep.tile([P, T], U8, name="xs")
         gt_sb = keep.tile([P, PACK], F32, name="gt_sb")
         tau_sb = keep.tile([P, N // P, 1], F32, name="tau_sb")
 
-        nc.vector.memset(xs[:].bitcast(I32), 0)
-        nc.sync.dma_start(wa_raw[:], wa.rearrange("(p j) n -> p j n", j=PACK))
+        wa_rows = wa.rearrange("(p j) n -> p j n", j=PACK)
+        w1_rows = w1.rearrange("(p j) n -> p j n", j=PACK)
+        nc.vector.memset(xs[:, 0 : T // 2].bitcast(I32), 0)
+        nc.gpsimd.memset(xs[:, T // 2 : T].bitcast(I32), 0)
+        x_rows = x_words[0].rearrange("p n r -> p (n r)").bitcast(I32)
+        nc.sync.dma_start(xw[:, 0 : T // 4], x_rows[:, 0 : T // 4])
         nc.sync.dma_start(offs_sb[:], offs)
+        nc.sync.dma_start(xw[:, T // 4 : T // 2], x_rows[:, T // 4 : T // 2])
         for q in range(4):
-            nc.scalar.dma_start(
+            nc.sync.dma_start(
                 xs[32 * q : 32 * q + 4, :].bitcast(I32), x_scales[0, 4 * q : 4 * q + 4, :].bitcast(I32)
             )
-        nc.sync.dma_start(xw[:], x_words[0].rearrange("p n r -> p (n r)").bitcast(I32))
+        nc.sync.dma_start(xw[:, T // 2 : T], x_rows[:, T // 2 : T])
+        for u in range(2):
+            nc.sync.dma_start(wa_raw[u][:], wa_rows[:, :, u * half : (u + 1) * half])
         nc.sync.dma_start(n3_sb[:], n3)
         nc.sync.dma_start(n1_sb[:], n1)
         nc.sync.dma_start(n2_sb[:], n2)
         nc.sync.dma_start(gt_sb[:], gt.rearrange("(p j) o -> p (j o)", j=PACK))
-        nc.sync.dma_start(w1_raw[:], w1.rearrange("(p j) n -> p j n", j=PACK))
+        nc.sync.dma_start(w1_first[:], w1_rows[:, :, 0:P])
+        nc.sync.dma_start(w1_rest[:], w1_rows[:, :, P:N])
         nc.sync.dma_start(n4_sb[:], n4)
         with nc.allow_non_contiguous_dma(reason="one rate for each partition and block of rows"):
             nc.sync.dma_start(tau_sb[:], tau.rearrange("(b p) o -> p b o", p=P))
@@ -76,175 +92,252 @@ def tile_picked_tokdotegp_none_p_kernel(
         xs_pick = keep.tile([P, S], U8, name="xs_pick", align_bytes=64)
         xw_pick = keep.tile([P, S], U32, name="xw_pick", align_bytes=64)
         nc.vector.tensor_copy(xs_pick[:].rearrange("p (t m) -> p m t", t=PACK), xs[:].indirect(offs_sb[:]))
-
-        wa_codes = keep.tile([P, H], U32, name="wa_codes", align_bytes=64)
-        wa_scales = keep.tile([P, H], U8, name="wa_scales", align_bytes=64)
-        half = H // 2
-        wa_lo = keep.tile([P, half, PACK], BF16, name="wa_lo", align_bytes=64)
-        wa_hi = keep.tile([P, half, PACK], BF16, name="wa_hi", align_bytes=64)
-        dst, src = weave_views(wa_lo[:], wa_raw[:, :, 0:half])
-        nc.vector.tensor_copy(dst, src)
-        dst, src = weave_views(wa_hi[:], wa_raw[:, :, half:H])
-        nc.scalar.activation(dst, src, ACT.Copy)
-        for first, woven in ((0, wa_lo), (half, wa_hi)):
-            nc.vector.quantize_mx(
-                out=wa_codes[:, first : first + half].bitcast(FP8X4),
-                scales=wa_scales[:, first : first + half],
-                in_=woven[:].rearrange("p n t -> p (n t)"),
-            )
         nc.vector.tensor_copy(
             xw_pick[:].rearrange("p (t m) -> p m t", t=PACK), xw[:].bitcast(U32).indirect(offs_sb[:])
         )
+
+        wa_codes = keep.tile([P, H], U32, name="wa_codes", align_bytes=64)
+        wa_scales = keep.tile([P, H], U8, name="wa_scales", align_bytes=64)
+        wa_woven = [keep.tile([P, half, PACK], BF16, name="wa_woven%d" % u, align_bytes=64) for u in range(2)]
+        dst, src = weave_views(wa_woven[0][:], wa_raw[0][:])
+        nc.scalar.activation(dst, src, ACT.Copy)
+        dst, src = weave_views(wa_woven[1][:], wa_raw[1][:])
+        nc.vector.tensor_copy(dst, src)
+        for u in range(2):
+            nc.vector.quantize_mx(
+                out=wa_codes[:, u * half : (u + 1) * half].bitcast(FP8X4),
+                scales=wa_scales[:, u * half : (u + 1) * half],
+                in_=wa_woven[u][:].rearrange("p n t -> p (n t)"),
+            )
         gain = keep.tile([P, PACK], F32, name="gain")
         nc.vector.tensor_scalar(gain[:], gt_sb[:], 0.75, None, ALU.mult)
 
-        y = []
-        for t in range(PACK):
-            bank = psum.tile([P, H], F32, name="y_bank%d" % t)
+        def first_product(bank, t, cols):
             nc.tensor.matmul_mx(
-                out=bank[:],
+                out=bank,
                 lhsT=xw_pick[:, t * P : (t + 1) * P].bitcast(FP8X4),
                 lhsT_scale=xs_pick[:, t * P : (t + 1) * P],
-                rhs=wa_codes[:].bitcast(FP8X4),
-                rhs_scale=wa_scales[:],
+                rhs=wa_codes[:, cols].bitcast(FP8X4),
+                rhs_scale=wa_scales[:, cols],
                 start=True,
                 stop=True,
             )
-            y_t = keep.tile([P, H], F32, name="y%d" % t)
-            if t in (1, 2):
-                nc.vector.tensor_copy(y_t[:], bank[:])
+
+        y = [keep.tile([P, H], F32, name="y%d" % t) for t in range(PACK)]
+        y0_lo = psum.tile([P, half], F32, name="y0_lo")
+        y0_hi = psum.tile([P, half], F32, name="y0_hi")
+        first_product(y0_lo[:], 0, slice(0, half))
+        first_product(y0_hi[:], 0, slice(half, H))
+        def evac(e, dst, src):
+            if e == "v":
+                nc.vector.tensor_copy(dst, src)
             else:
-                nc.scalar.activation(y_t[:], bank[:], ACT.Copy)
-            y.append(y_t)
+                nc.scalar.activation(dst, src, ACT.Copy)
+
+        evac(YENG[0], y[0][:, 0:half], y0_lo[:])
+        evac(YENG[1], y[0][:, half:H], y0_hi[:])
+        for t in range(1, PACK):
+            bank = psum.tile([P, H], F32, name="bank%d" % t)
+            first_product(bank[:], t, slice(0, H))
+            evac(YENG[t + 1], y[t][:], bank[:])
 
         h = [keep.tile([P, 2 * H], F32, name="h%d" % b) for b in range(N // P)]
         z_codes = keep.tile([P, H], U32, name="z_codes", align_bytes=64)
         z_scales = keep.tile([P, H], U8, name="z_scales", align_bytes=64)
-        w1_codes = [keep.tile([P, P], U32, name="w1_codes%d" % b, align_bytes=64) for b in range(N // P)]
-        w1_scales = [keep.tile([P, P], U8, name="w1_scales%d" % b, align_bytes=64) for b in range(N // P)]
-        w1_woven = [keep.tile([P, P, PACK], BF16, name="w1_woven%d" % b, align_bytes=64) for b in range(N // P)]
+        w1_raw = (w1_first, w1_rest)
+        w1_codes = [keep.tile([P, n], U32, name="w1_codes%d" % n, align_bytes=64) for n in (P, N - P)]
+        w1_scales = [keep.tile([P, n], U8, name="w1_scales%d" % n, align_bytes=64) for n in (P, N - P)]
+        w1_woven = [keep.tile([P, P, PACK], BF16, name="w1_woven_first", align_bytes=64)]
 
-        def round_w1(b):
-            dst, src = weave_views(w1_woven[b][:], w1_raw[:, :, b * P : (b + 1) * P])
+        def round_w1(part):
+            dst, src = weave_views(w1_woven[part][:], w1_raw[part][:])
             nc.scalar.activation(dst, src, ACT.Copy)
 
-        def quantize_w1(b):
+        def quantize_w1(part):
             nc.vector.quantize_mx(
-                out=w1_codes[b][:].bitcast(FP8X4),
-                scales=w1_scales[b][:],
-                in_=w1_woven[b][:].rearrange("p n t -> p (n t)"),
+                out=w1_codes[part][:].bitcast(FP8X4),
+                scales=w1_scales[part][:],
+                in_=w1_woven[part][:].rearrange("p n t -> p (n t)"),
             )
 
-        chunks = []
-        for chunk, (first, width) in enumerate(Z_CHUNKS):
-            cols = slice(first, first + width)
-            z_planes = keep.tile([P, PACK, width], BF16, name="z_planes%d" % chunk, align_bytes=64)
-            z_woven = keep.tile([P, width, PACK], BF16, name="z_woven%d" % chunk, align_bytes=64)
-            pending = None
-            for t in range(PACK):
-                y3 = keep.tile([P, width], F32, name="y3_%d_%d" % (chunk, t))
-                y1 = keep.tile([P, width], F32, name="y1_%d_%d" % (chunk, t))
-                cross = keep.tile([P, width], F32, name="cross_%d_%d" % (chunk, t))
-                own = h[t][:, H + first : H + first + width]
-                nc.scalar.activation(y3[:], y[t][:].indirect(entries(n3_sb, first, width)), ACT.Copy)
-                nc.scalar.activation(y1[:], y[t][:].indirect(entries(n1_sb, first, width)), ACT.Copy)
-                nc.vector.tensor_tensor(cross[:], y[t][:].indirect(entries(n2_sb, first, width)), y3[:], ALU.mult)
-                if pending is not None:
-                    nc.vector.scalar_tensor_tensor(*pending, ALU.mult, ALU.add)
-                nc.vector.scalar_tensor_tensor(own, y1[:], gain[:, t : t + 1], y[t][:, cols], ALU.mult, ALU.mult)
-                pending = (z_planes[:, t, :], cross[:], gain[:, t : t + 1], own)
-            nc.vector.scalar_tensor_tensor(*pending, ALU.mult, ALU.add)
-            chunks.append((cols, z_planes, z_woven))
-        round_w1(0)
-        for chunk, (cols, z_planes, z_woven) in enumerate(chunks):
-            dst, src = weave_views(z_woven[:], z_planes[:])
-            if chunk == 0:
-                nc.scalar.copy(dst, src)
-            else:
-                nc.vector.tensor_copy(dst, src)
-        quantize_w1(0)
-        for cols, z_planes, z_woven in chunks:
+        def look_up(dst, t, offsets, first, width):
+            nc.scalar.activation(dst, y[t][:].indirect(entries(offsets, first, width)), ACT.Copy)
+
+        def quantize_z(cols, z_woven):
             nc.vector.quantize_mx(
                 out=z_codes[:, cols].bitcast(FP8X4),
                 scales=z_scales[:, cols],
                 in_=z_woven[:].rearrange("p n t -> p (n t)"),
             )
 
+        for chunk, (first, width, engine) in enumerate(Z_CHUNKS):
+            cols = slice(first, first + width)
+            z_woven = keep.tile([P, width, PACK], BF16, name="z_woven%d" % chunk, align_bytes=64)
+            if engine == "vector":
+                z_planes = keep.tile([P, PACK, width], BF16, name="z_planes%d" % chunk, align_bytes=64)
+                pending = None
+                for t in range(PACK):
+                    y3 = keep.tile([P, width], F32, name="y3_%d_%d" % (chunk, t), align_bytes=64)
+                    y1 = keep.tile([P, width], F32, name="y1_%d_%d" % (chunk, t))
+                    cross = keep.tile([P, width], F32, name="cross_%d_%d" % (chunk, t))
+                    own = h[t][:, H + first : H + first + width]
+                    look_up(y3[:], t, n3_sb, first, width)
+                    look_up(y1[:], t, n1_sb, first, width)
+                    nc.vector.tensor_tensor(
+                        cross[:], y[t][:].indirect(entries(n2_sb, first, width)), y3[:], ALU.mult
+                    )
+                    if pending is not None:
+                        nc.vector.scalar_tensor_tensor(*pending, ALU.mult, ALU.add)
+                    nc.vector.scalar_tensor_tensor(
+                        own, y1[:], gain[:, t : t + 1], y[t][:, cols], ALU.mult, ALU.mult
+                    )
+                    pending = (z_planes[:, t, :], cross[:], gain[:, t : t + 1], own)
+                nc.vector.scalar_tensor_tensor(*pending, ALU.mult, ALU.add)
+                if chunk == 0:
+                    round_w1(0)
+                dst, src = weave_views(z_woven[:], z_planes[:])
+                nc.vector.tensor_copy(dst, src)
+                if chunk == 0:
+                    quantize_w1(0)
+                quantize_z(cols, z_woven)
+            else:
+                owns = keep.tile([P, PACK, width], F32, name="owns%d" % chunk)
+                crosses = keep.tile([P, PACK, width], F32, name="crosses%d" % chunk)
+                for t in range(PACK):
+                    y3 = keep.tile([P, width], F32, name="y3_%d_%d" % (chunk, t))
+                    y1 = keep.tile([P, width], F32, name="y1_%d_%d" % (chunk, t))
+                    y2 = h[t][:, H + first : H + first + width]
+                    look_up(y3[:], t, n3_sb, first, width)
+                    look_up(y2, t, n2_sb, first, width)
+                    look_up(y1[:], t, n1_sb, first, width)
+                    nc.vector.scalar_tensor_tensor(
+                        crosses[:, t, :], y2, gain[:, t : t + 1], y3[:], ALU.mult, ALU.mult
+                    )
+                    nc.vector.scalar_tensor_tensor(
+                        owns[:, t, :], y1[:], gain[:, t : t + 1], y[t][:, cols], ALU.mult, ALU.mult
+                    )
+                dst, src0 = weave_views(z_woven[:], crosses[:])
+                dst, src1 = weave_views(z_woven[:], owns[:])
+                nc.vector.tensor_tensor(dst, src0, src1, ALU.add)
+                quantize_z(cols, z_woven)
+
         scale_bias = []
 
-        def second_product(b):
-            bank = psum.tile([P, H], F32, name="h_bank%d" % b)
-            for first, width in ((0, 256), (256, 128), (384, 128)):
-                cols = slice(first, first + width)
-                nc.tensor.matmul_mx(
-                    out=bank[:, cols],
-                    lhsT=w1_codes[b][:].bitcast(FP8X4),
-                    lhsT_scale=w1_scales[b][:],
-                    rhs=z_codes[:, cols].bitcast(FP8X4),
-                    rhs_scale=z_scales[:, cols],
-                    start=True,
-                    stop=True,
-                )
-            top = keep.tile([P, 1], F32, name="top%d" % b)
-            bias = keep.tile([P, 1], F32, name="bias%d" % b)
-            nc.vector.tensor_scalar(h[b][:, 0:H], bank[:], 1.0, None, ALU.mult, ALU.max, accum_out=top[:])
-            nc.vector.tensor_scalar(bias[:], top[:], tau_sb[:, b, :], -1.0, ALU.mult, ALU.mult)
-            scale_bias.append((tau_sb[:, b, :], bias[:]))
+        def product_into(bank, b, cols):
+            part, rows = (0, slice(0, P)) if b == 0 else (1, slice((b - 1) * P, b * P))
+            nc.tensor.matmul_mx(
+                out=bank,
+                lhsT=w1_codes[part][:, rows].bitcast(FP8X4),
+                lhsT_scale=w1_scales[part][:, rows],
+                rhs=z_codes[:, cols].bitcast(FP8X4),
+                rhs_scale=z_scales[:, cols],
+                start=True,
+                stop=True,
+            )
 
-        second_product(0)
+        top0 = keep.tile([P, 1], F32, name="top0")
+        bias0 = keep.tile([P, 1], F32, name="bias0")
+        early = psum.tile([P, 384], F32, name="h0_early")
+        late = psum.tile([P, 128], F32, name="h0_late")
+        early_top = keep.tile([P, 1], F32, name="early_top")
+        product_into(early[:, 0:256], 0, slice(0, 256))
+        product_into(early[:, 256:384], 0, slice(256, 384))
+        product_into(late[:], 0, slice(384, H))
+        nc.vector.tensor_scalar(h[0][:, 0:384], early[:], 1.0, None, ALU.mult, ALU.max, accum_out=early_top[:])
+        nc.vector.tensor_scalar(h[0][:, 384:H], late[:], 1.0, early_top[:], ALU.mult, ALU.max, accum_out=top0[:])
+        nc.vector.tensor_scalar(bias0[:], top0[:], tau_sb[:, 0, :], -1.0, ALU.mult, ALU.mult)
+        scale_bias.append((tau_sb[:, 0, :], bias0[:]))
+
+        w1_woven.append(keep.tile([P, N - P, PACK], BF16, name="w1_woven_rest", tag="y3_0_2", align_bytes=64))
+        round_w1(1)
+        if QSPLIT:
+            for b in range(3):
+                nc.vector.quantize_mx(
+                    out=w1_codes[1][:, b * P : (b + 1) * P].bitcast(FP8X4),
+                    scales=w1_scales[1][:, b * P : (b + 1) * P],
+                    in_=w1_woven[1][:, b * P : (b + 1) * P, :].rearrange("p n t -> p (n t)"),
+                )
+        else:
+            quantize_w1(1)
+        tops = keep.tile([P, N // P - 1], F32, name="tops")
+        biases = keep.tile([P, N // P - 1], F32, name="biases")
         for b in range(1, N // P):
-            round_w1(b)
-            quantize_w1(b)
-            second_product(b)
+            bank = psum.tile([P, H], F32, name="bank%d" % b)
+            product_into(bank[:], b, slice(0, H))
+            nc.vector.tensor_scalar(
+                h[b][:, 0:H], bank[:], 1.0, None, ALU.mult, ALU.max, accum_out=tops[:, b - 1 : b]
+            )
+            scale_bias.append((tau_sb[:, b, :], biases[:, b - 1 : b]))
+        nc.vector.scalar_tensor_tensor(biases[:], tops[:], -1.0, tau_sb[:, 1:, 0], ALU.mult, ALU.mult)
 
         pieces = []
-        for b in range(N // P):
-            widths = ((128, 128, 256), (256, 256), (256, 256), (256, 128, 128))[b]
-            first = 0
-            for width in widths:
-                pieces.append((b, first, width))
-                first = first + width
+        f0 = 0
+        for wd in FIRST:
+            pieces.append((0, f0, wd, (f0, wd)))
+            f0 = f0 + wd
+        for b in range(1, N // P - 1):
+            pieces.extend([(b, 0, 256, None if MID else (0, 256)), (b, 256, 256, (0, 512) if MID else (256, 256))])
+        last = N // P - 1
+        f0 = 0
+        for wd in LAST:
+            pieces.append((last, f0, wd, (f0, wd)))
+            f0 = f0 + wd
+
+        mx = [keep.tile([P, H], F32, name="mx%d" % b) for b in range(N // P)]
+        mn = [keep.tile([P, H], F32, name="mn%d" % b) for b in range(N // P)]
+        spread = [keep.tile([P, H], F32, name="spread%d" % b) for b in range(N // P)]
+
+        def finish_sub(b, cols):
+            nc.vector.tensor_tensor(spread[b][:, cols], mx[b][:, cols], mn[b][:, cols], ALU.subtract)
+
+        def finish_out(b, cols):
+            result = keep.tile([P, cols.stop - cols.start], F32, name="result_%d_%d" % (b, cols.start))
+            nc.vector.scalar_tensor_tensor(result[:], spread[b][:, cols], 3.0, h[b][:, cols], ALU.mult, ALU.mult)
+            nc.sync.dma_start(out[b * P : (b + 1) * P, cols], result[:])
 
         previous = None
-
-        def finish_sub(state):
-            b, first, width, mx, mn, spread = state
-            nc.vector.tensor_tensor(spread[:], mx[:], mn[:], ALU.subtract)
-
-        def finish_out(state):
-            b, first, width, mx, mn, spread = state
-            result = keep.tile([P, width], F32, name="result_%d_%d" % (b, first))
-            nc.vector.scalar_tensor_tensor(
-                result[:], spread[:], 3.0, h[b][:, first : first + width], ALU.mult, ALU.mult
-            )
-            nc.sync.dma_start(out[b * P : (b + 1) * P, first : first + width], result[:])
-
-        for b, first, width in pieces:
+        for b, first, width, stretch in pieces:
             scale, bias = scale_bias[b]
             name = "_%d_%d" % (b, first)
+            cols = slice(first, first + width)
             ea = keep.tile([P, width, MEMBERS], F32, name="ea" + name)
             flat = ea[:].rearrange("p j t -> p (j t)")
-            for e0 in range(0, width * MEMBERS, EXP_OFFSETS):
+            step = min(EXP_OFFSETS, width * MEMBERS)
+            for e0 in range(0, width * MEMBERS, step):
                 nc.scalar.activation(
-                    flat[:, e0 : e0 + EXP_OFFSETS],
-                    h[b][:].indirect(entries(n4_sb, first * MEMBERS + e0, EXP_OFFSETS)),
+                    flat[:, e0 : e0 + step],
+                    h[b][:].indirect(entries(n4_sb, first * MEMBERS + e0, step)),
                     ACT.Exp,
                     bias=bias,
                     scale=scale,
                 )
             upper = keep.tile([P, width, 2], F32, name="upper" + name)
             lower = keep.tile([P, width, 2], F32, name="lower" + name)
-            mx = keep.tile([P, width], F32, name="mx" + name)
-            mn = keep.tile([P, width], F32, name="mn" + name)
-            spread = keep.tile([P, width], F32, name="spread" + name)
             nc.vector.tensor_tensor(upper[:], ea[:, :, 0:2], ea[:, :, 2:4], ALU.max)
             nc.vector.tensor_tensor(lower[:], ea[:, :, 0:2], ea[:, :, 2:4], ALU.min)
-            if previous is not None:
-                finish_sub(previous)
-            nc.vector.tensor_tensor(mx[:], upper[:, :, 0], upper[:, :, 1], ALU.max)
-            if previous is not None:
-                finish_out(previous)
-            nc.vector.tensor_tensor(mn[:], lower[:, :, 0], lower[:, :, 1], ALU.min)
-            previous = (b, first, width, mx, mn, spread)
-        finish_sub(previous)
-        finish_out(previous)
+            now = None if stretch is None else (b, slice(stretch[0], stretch[0] + stretch[1]))
+            if ORDER == 0:
+                if previous is not None:
+                    finish_sub(*previous)
+                nc.vector.tensor_tensor(mx[b][:, cols], upper[:, :, 0], upper[:, :, 1], ALU.max)
+                if previous is not None:
+                    finish_out(*previous)
+                nc.vector.tensor_tensor(mn[b][:, cols], lower[:, :, 0], lower[:, :, 1], ALU.min)
+            elif ORDER == 1:
+                nc.vector.tensor_tensor(mx[b][:, cols], upper[:, :, 0], upper[:, :, 1], ALU.max)
+                nc.vector.tensor_tensor(mn[b][:, cols], lower[:, :, 0], lower[:, :, 1], ALU.min)
+                if previous is not None:
+                    finish_out(*previous)
+                if now is not None:
+                    finish_sub(*now)
+            else:
+                nc.vector.tensor_tensor(mx[b][:, cols], upper[:, :, 0], upper[:, :, 1], ALU.max)
+                nc.vector.tensor_tensor(mn[b][:, cols], lower[:, :, 0], lower[:, :, 1], ALU.min)
+                if now is not None:
+                    finish_sub(*now)
+                    finish_out(*now)
+            previous = now
+        if ORDER == 0:
+            finish_sub(*previous)
+        if ORDER < 2:
+            finish_out(*previous)

@@ -17,16 +17,14 @@ ACT = mybir.ActivationFunctionType
 
 P = 128
 PACK = 4
+BLOCKS = N // P
 LIST_ROWS = 16
-MEMBERS = 4
-Z_CHUNKS = ((0, 384, 'vector'), (384, 128, 'scalar'))
-YENG = 'svvsv'
-LAST = (256, 256)
-MID = False
-ORDER = 1
-FIRST = (128, 128, 256)
-QSPLIT = True
-EXP_OFFSETS = 512
+MEMBERS = W // H
+HALF = H // 2
+Y_SPARE = 32
+Z_PARTS = ((0, 256), (256, 128), (384, 128))
+EARLY = Z_PARTS[-1][0]
+PIECE = 256
 
 
 def weave_views(woven, planes):
@@ -38,6 +36,22 @@ def weave_views(woven, planes):
 
 def entries(offsets, first, count):
     return offsets[:, first // LIST_ROWS : (first + count) // LIST_ROWS]
+
+
+def quantize(nc, codes, scales, woven):
+    nc.vector.quantize_mx(out=codes.bitcast(FP8X4), scales=scales, in_=woven.rearrange("p n t -> p (n t)"))
+
+
+def mx_product(nc, bank, lhs_codes, lhs_scales, rhs_codes, rhs_scales):
+    nc.tensor.matmul_mx(
+        out=bank,
+        lhsT=lhs_codes.bitcast(FP8X4),
+        lhsT_scale=lhs_scales,
+        rhs=rhs_codes.bitcast(FP8X4),
+        rhs_scale=rhs_scales,
+        start=True,
+        stop=True,
+    )
 
 
 def tile_picked_tokdotegp_none_p_kernel(
@@ -55,14 +69,13 @@ def tile_picked_tokdotegp_none_p_kernel(
         n3_sb = lists.tile([P, H // LIST_ROWS], U16, name="n3_sb")
         n4_sb = lists.tile([P, W // LIST_ROWS], U16, name="n4_sb")
 
-        half = H // 2
-        wa_raw = [keep.tile([P, PACK, half], F32, name="wa_raw%d" % u) for u in range(2)]
-        w1_first = keep.tile([P, PACK, P], F32, name="w1_first")
-        w1_rest = keep.tile([P, PACK, N - P], F32, name="w1_rest")
+        wa_raw = [keep.tile([P, PACK, HALF], F32, name="wa_raw%d" % u) for u in range(2)]
+        w1_first_raw = keep.tile([P, PACK, P], F32, name="w1_first_raw")
+        w1_rest_raw = keep.tile([P, PACK, N - P], F32, name="w1_rest_raw")
         xw = keep.tile([P, T], I32, name="xw")
         xs = keep.tile([P, T], U8, name="xs")
         gt_sb = keep.tile([P, PACK], F32, name="gt_sb")
-        tau_sb = keep.tile([P, N // P, 1], F32, name="tau_sb")
+        tau_sb = keep.tile([P, BLOCKS, 1], F32, name="tau_sb")
 
         wa_rows = wa.rearrange("(p j) n -> p j n", j=PACK)
         w1_rows = w1.rearrange("(p j) n -> p j n", j=PACK)
@@ -78,15 +91,15 @@ def tile_picked_tokdotegp_none_p_kernel(
             )
         nc.sync.dma_start(xw[:, T // 2 : T], x_rows[:, T // 2 : T])
         for u in range(2):
-            nc.sync.dma_start(wa_raw[u][:], wa_rows[:, :, u * half : (u + 1) * half])
+            nc.sync.dma_start(wa_raw[u][:], wa_rows[:, :, u * HALF : (u + 1) * HALF])
+        nc.sync.dma_start(w1_first_raw[:], w1_rows[:, :, 0:P])
         nc.sync.dma_start(n3_sb[:], n3)
         nc.sync.dma_start(n1_sb[:], n1)
         nc.sync.dma_start(n2_sb[:], n2)
         nc.sync.dma_start(gt_sb[:], gt.rearrange("(p j) o -> p (j o)", j=PACK))
-        nc.sync.dma_start(w1_first[:], w1_rows[:, :, 0:P])
-        nc.sync.dma_start(w1_rest[:], w1_rows[:, :, P:N])
+        nc.sync.dma_start(w1_rest_raw[:], w1_rows[:, :, P:N])
         nc.sync.dma_start(n4_sb[:], n4)
-        with nc.allow_non_contiguous_dma(reason="one rate for each partition and block of rows"):
+        with nc.allow_non_contiguous_dma(reason="one rate for each partition and row block"):
             nc.sync.dma_start(tau_sb[:], tau.rearrange("(b p) o -> p b o", p=P))
 
         xs_pick = keep.tile([P, S], U8, name="xs_pick", align_bytes=64)
@@ -98,246 +111,172 @@ def tile_picked_tokdotegp_none_p_kernel(
 
         wa_codes = keep.tile([P, H], U32, name="wa_codes", align_bytes=64)
         wa_scales = keep.tile([P, H], U8, name="wa_scales", align_bytes=64)
-        wa_woven = [keep.tile([P, half, PACK], BF16, name="wa_woven%d" % u, align_bytes=64) for u in range(2)]
-        dst, src = weave_views(wa_woven[0][:], wa_raw[0][:])
-        nc.scalar.activation(dst, src, ACT.Copy)
-        dst, src = weave_views(wa_woven[1][:], wa_raw[1][:])
-        nc.vector.tensor_copy(dst, src)
+        wa_woven = [keep.tile([P, HALF, PACK], BF16, name="wa_woven%d" % u, align_bytes=64) for u in range(2)]
+        nc.scalar.activation(*weave_views(wa_woven[0][:], wa_raw[0][:]), ACT.Copy)
+        nc.vector.tensor_copy(*weave_views(wa_woven[1][:], wa_raw[1][:]))
         for u in range(2):
-            nc.vector.quantize_mx(
-                out=wa_codes[:, u * half : (u + 1) * half].bitcast(FP8X4),
-                scales=wa_scales[:, u * half : (u + 1) * half],
-                in_=wa_woven[u][:].rearrange("p n t -> p (n t)"),
-            )
-        gain = keep.tile([P, PACK], F32, name="gain")
-        nc.vector.tensor_scalar(gain[:], gt_sb[:], 0.75, None, ALU.mult)
+            cols = slice(u * HALF, (u + 1) * HALF)
+            quantize(nc, wa_codes[:, cols], wa_scales[:, cols], wa_woven[u][:])
+
+        w1_first_codes = keep.tile([P, P], U32, name="w1_first_codes", align_bytes=64)
+        w1_rest_codes = keep.tile([P, N - P], U32, name="w1_rest_codes", align_bytes=64)
+        w1_first_scales = keep.tile([P, P], U8, name="w1_first_scales", align_bytes=64)
+        w1_first_woven = keep.tile([P, P, PACK], BF16, name="w1_first_woven", align_bytes=64)
+        nc.scalar.activation(*weave_views(w1_first_woven[:], w1_first_raw[:]), ACT.Copy)
 
         def first_product(bank, t, cols):
-            nc.tensor.matmul_mx(
-                out=bank,
-                lhsT=xw_pick[:, t * P : (t + 1) * P].bitcast(FP8X4),
-                lhsT_scale=xs_pick[:, t * P : (t + 1) * P],
-                rhs=wa_codes[:, cols].bitcast(FP8X4),
-                rhs_scale=wa_scales[:, cols],
-                start=True,
-                stop=True,
-            )
+            tokens = slice(t * P, (t + 1) * P)
+            mx_product(nc, bank, xw_pick[:, tokens], xs_pick[:, tokens], wa_codes[:, cols], wa_scales[:, cols])
 
-        y = [keep.tile([P, H], F32, name="y%d" % t) for t in range(PACK)]
-        y0_lo = psum.tile([P, half], F32, name="y0_lo")
-        y0_hi = psum.tile([P, half], F32, name="y0_hi")
-        first_product(y0_lo[:], 0, slice(0, half))
-        first_product(y0_hi[:], 0, slice(half, H))
-        def evac(e, dst, src):
-            if e == "v":
-                nc.vector.tensor_copy(dst, src)
-            else:
-                nc.scalar.activation(dst, src, ACT.Copy)
-
-        evac(YENG[0], y[0][:, 0:half], y0_lo[:])
-        evac(YENG[1], y[0][:, half:H], y0_hi[:])
+        y = [keep.tile([P, H + Y_SPARE], F32, name="y%d" % t) for t in range(PACK)]
+        y0_low = psum.tile([P, HALF], F32, name="y0_low")
+        y0_high = psum.tile([P, HALF], F32, name="y0_high")
+        first_product(y0_low[:], 0, slice(0, HALF))
+        first_product(y0_high[:], 0, slice(HALF, H))
+        nc.scalar.activation(y[0][:, 0:HALF], y0_low[:], ACT.Copy)
+        nc.vector.tensor_copy(y[0][:, HALF:H], y0_high[:])
         for t in range(1, PACK):
             bank = psum.tile([P, H], F32, name="bank%d" % t)
             first_product(bank[:], t, slice(0, H))
-            evac(YENG[t + 1], y[t][:], bank[:])
+            if t == PACK - 1:
+                gain = keep.tile([P, PACK], F32, name="gain", tag="wa_scales", align_bytes=64)
+                nc.vector.tensor_scalar(gain[:], gt_sb[:], 0.75, None, ALU.mult)
+            nc.vector.tensor_copy(y[t][:, 0:H], bank[:])
 
-        h = [keep.tile([P, 2 * H], F32, name="h%d" % b) for b in range(N // P)]
+        wide = [keep.tile([P, 4 * H], F32, name="wide%d" % n) for n in range(BLOCKS)]
         z_codes = keep.tile([P, H], U32, name="z_codes", align_bytes=64)
         z_scales = keep.tile([P, H], U8, name="z_scales", align_bytes=64)
-        w1_raw = (w1_first, w1_rest)
-        w1_codes = [keep.tile([P, n], U32, name="w1_codes%d" % n, align_bytes=64) for n in (P, N - P)]
-        w1_scales = [keep.tile([P, n], U8, name="w1_scales%d" % n, align_bytes=64) for n in (P, N - P)]
-        w1_woven = [keep.tile([P, P, PACK], BF16, name="w1_woven_first", align_bytes=64)]
-
-        def round_w1(part):
-            dst, src = weave_views(w1_woven[part][:], w1_raw[part][:])
-            nc.scalar.activation(dst, src, ACT.Copy)
-
-        def quantize_w1(part):
-            nc.vector.quantize_mx(
-                out=w1_codes[part][:].bitcast(FP8X4),
-                scales=w1_scales[part][:],
-                in_=w1_woven[part][:].rearrange("p n t -> p (n t)"),
-            )
+        z_planes = keep.tile([P, PACK, H], BF16, name="z_planes", align_bytes=64)
+        z_woven = [keep.tile([P, n, PACK], BF16, name="z_woven%d" % f, align_bytes=64) for f, n in Z_PARTS]
+        cross = keep.tile([P, PACK * H], F32, name="cross", tag="wa_codes", align_bytes=64)
 
         def look_up(dst, t, offsets, first, width):
             nc.scalar.activation(dst, y[t][:].indirect(entries(offsets, first, width)), ACT.Copy)
 
-        def quantize_z(cols, z_woven):
-            nc.vector.quantize_mx(
-                out=z_codes[:, cols].bitcast(FP8X4),
-                scales=z_scales[:, cols],
-                in_=z_woven[:].rearrange("p n t -> p (n t)"),
+        def plane(t, n, first, width):
+            return wide[t][:, n * H + first : n * H + first + width]
+
+        def cross_of(t, first, width):
+            return cross[:, t * H + first : t * H + first + width]
+
+        def make_cross(t, first, width):
+            look_up(plane(t, 2, first, width), t, n3_sb, first, width)
+            look_up(plane(t, 3, first, width), t, n1_sb, first, width)
+            nc.vector.tensor_tensor(
+                cross_of(t, first, width),
+                y[t][:].indirect(entries(n2_sb, first, width)),
+                plane(t, 2, first, width),
+                ALU.mult,
             )
 
-        for chunk, (first, width, engine) in enumerate(Z_CHUNKS):
-            cols = slice(first, first + width)
-            z_woven = keep.tile([P, width, PACK], BF16, name="z_woven%d" % chunk, align_bytes=64)
-            if engine == "vector":
-                z_planes = keep.tile([P, PACK, width], BF16, name="z_planes%d" % chunk, align_bytes=64)
-                pending = None
-                for t in range(PACK):
-                    y3 = keep.tile([P, width], F32, name="y3_%d_%d" % (chunk, t), align_bytes=64)
-                    y1 = keep.tile([P, width], F32, name="y1_%d_%d" % (chunk, t))
-                    cross = keep.tile([P, width], F32, name="cross_%d_%d" % (chunk, t))
-                    own = h[t][:, H + first : H + first + width]
-                    look_up(y3[:], t, n3_sb, first, width)
-                    look_up(y1[:], t, n1_sb, first, width)
-                    nc.vector.tensor_tensor(
-                        cross[:], y[t][:].indirect(entries(n2_sb, first, width)), y3[:], ALU.mult
-                    )
-                    if pending is not None:
-                        nc.vector.scalar_tensor_tensor(*pending, ALU.mult, ALU.add)
-                    nc.vector.scalar_tensor_tensor(
-                        own, y1[:], gain[:, t : t + 1], y[t][:, cols], ALU.mult, ALU.mult
-                    )
-                    pending = (z_planes[:, t, :], cross[:], gain[:, t : t + 1], own)
-                nc.vector.scalar_tensor_tensor(*pending, ALU.mult, ALU.add)
-                if chunk == 0:
-                    round_w1(0)
-                dst, src = weave_views(z_woven[:], z_planes[:])
-                nc.vector.tensor_copy(dst, src)
-                if chunk == 0:
-                    quantize_w1(0)
-                quantize_z(cols, z_woven)
+        def make_own(t, first, width):
+            nc.vector.scalar_tensor_tensor(
+                plane(t, 1, first, width),
+                plane(t, 3, first, width),
+                gain[:, t : t + 1],
+                y[t][:, first : first + width],
+                ALU.mult,
+                ALU.mult,
+            )
+
+        def make_z(t, first, width):
+            nc.vector.scalar_tensor_tensor(
+                z_planes[:, t, first : first + width],
+                cross_of(t, first, width),
+                gain[:, t : t + 1],
+                plane(t, 1, first, width),
+                ALU.mult,
+                ALU.add,
+            )
+
+        def weave_z(part):
+            first, width = Z_PARTS[part]
+            views = weave_views(z_woven[part][:], z_planes[:, :, first : first + width])
+            if part == 0:
+                nc.scalar.copy(*views)
             else:
-                owns = keep.tile([P, PACK, width], F32, name="owns%d" % chunk)
-                crosses = keep.tile([P, PACK, width], F32, name="crosses%d" % chunk)
-                for t in range(PACK):
-                    y3 = keep.tile([P, width], F32, name="y3_%d_%d" % (chunk, t))
-                    y1 = keep.tile([P, width], F32, name="y1_%d_%d" % (chunk, t))
-                    y2 = h[t][:, H + first : H + first + width]
-                    look_up(y3[:], t, n3_sb, first, width)
-                    look_up(y2, t, n2_sb, first, width)
-                    look_up(y1[:], t, n1_sb, first, width)
-                    nc.vector.scalar_tensor_tensor(
-                        crosses[:, t, :], y2, gain[:, t : t + 1], y3[:], ALU.mult, ALU.mult
-                    )
-                    nc.vector.scalar_tensor_tensor(
-                        owns[:, t, :], y1[:], gain[:, t : t + 1], y[t][:, cols], ALU.mult, ALU.mult
-                    )
-                dst, src0 = weave_views(z_woven[:], crosses[:])
-                dst, src1 = weave_views(z_woven[:], owns[:])
-                nc.vector.tensor_tensor(dst, src0, src1, ALU.add)
-                quantize_z(cols, z_woven)
+                nc.vector.tensor_copy(*views)
 
-        scale_bias = []
+        def quantize_z(part):
+            first, width = Z_PARTS[part]
+            cols = slice(first, first + width)
+            quantize(nc, z_codes[:, cols], z_scales[:, cols], z_woven[part][:])
 
-        def product_into(bank, b, cols):
-            part, rows = (0, slice(0, P)) if b == 0 else (1, slice((b - 1) * P, b * P))
-            nc.tensor.matmul_mx(
-                out=bank,
-                lhsT=w1_codes[part][:, rows].bitcast(FP8X4),
-                lhsT_scale=w1_scales[part][:, rows],
-                rhs=z_codes[:, cols].bitcast(FP8X4),
-                rhs_scale=z_scales[:, cols],
-                start=True,
-                stop=True,
-            )
+        steps = [(t, 0, H) for t in range(PACK - 1)] + [(PACK - 1, first, width) for first, width in Z_PARTS]
+        for n, step in enumerate(steps):
+            make_cross(*step)
+            if n > 0:
+                make_z(*steps[n - 1])
+            make_own(*step)
+            if n == 0:
+                quantize(nc, w1_first_codes[:], w1_first_scales[:], w1_first_woven[:])
+            done = n - PACK
+            if done > 0:
+                quantize_z(done - 1)
+            if done >= 0:
+                weave_z(done)
+        last = len(Z_PARTS) - 1
+        make_z(*steps[-1])
+        quantize_z(last - 1)
+        weave_z(last)
+        quantize_z(last)
 
-        top0 = keep.tile([P, 1], F32, name="top0")
+        h = [wide[b][:, 0:H] for b in range(BLOCKS)]
+        top0 = keep.tile([P, 1], F32, name="top0", align_bytes=64)
         bias0 = keep.tile([P, 1], F32, name="bias0")
-        early = psum.tile([P, 384], F32, name="h0_early")
-        late = psum.tile([P, 128], F32, name="h0_late")
+        early = psum.tile([P, EARLY], F32, name="h0_early")
+        late = psum.tile([P, H - EARLY], F32, name="h0_late")
         early_top = keep.tile([P, 1], F32, name="early_top")
-        product_into(early[:, 0:256], 0, slice(0, 256))
-        product_into(early[:, 256:384], 0, slice(256, 384))
-        product_into(late[:], 0, slice(384, H))
-        nc.vector.tensor_scalar(h[0][:, 0:384], early[:], 1.0, None, ALU.mult, ALU.max, accum_out=early_top[:])
-        nc.vector.tensor_scalar(h[0][:, 384:H], late[:], 1.0, early_top[:], ALU.mult, ALU.max, accum_out=top0[:])
+        for first, width in Z_PARTS:
+            cols = slice(first, first + width)
+            bank_cols = early[:, cols] if first < EARLY else late[:]
+            mx_product(nc, bank_cols, w1_first_codes[:], w1_first_scales[:], z_codes[:, cols], z_scales[:, cols])
+        nc.vector.tensor_scalar(h[0][:, 0:EARLY], early[:], 1.0, None, ALU.mult, ALU.max, accum_out=early_top[:])
+        nc.vector.tensor_scalar(h[0][:, EARLY:H], late[:], 1.0, early_top[:], ALU.mult, ALU.max, accum_out=top0[:])
         nc.vector.tensor_scalar(bias0[:], top0[:], tau_sb[:, 0, :], -1.0, ALU.mult, ALU.mult)
-        scale_bias.append((tau_sb[:, 0, :], bias0[:]))
 
-        w1_woven.append(keep.tile([P, N - P, PACK], BF16, name="w1_woven_rest", tag="y3_0_2", align_bytes=64))
-        round_w1(1)
-        if QSPLIT:
-            for b in range(3):
-                nc.vector.quantize_mx(
-                    out=w1_codes[1][:, b * P : (b + 1) * P].bitcast(FP8X4),
-                    scales=w1_scales[1][:, b * P : (b + 1) * P],
-                    in_=w1_woven[1][:, b * P : (b + 1) * P, :].rearrange("p n t -> p (n t)"),
-                )
-        else:
-            quantize_w1(1)
-        tops = keep.tile([P, N // P - 1], F32, name="tops")
-        biases = keep.tile([P, N // P - 1], F32, name="biases")
-        for b in range(1, N // P):
+        w1_rest_woven = keep.tile([P, N - P, PACK], BF16, name="w1_rest_woven", tag="wa_codes", align_bytes=64)
+        w1_rest_scales = keep.tile([P, N - P], U8, name="w1_rest_scales", tag="top0", align_bytes=64)
+        nc.scalar.activation(*weave_views(w1_rest_woven[:], w1_rest_raw[:]), ACT.Copy)
+        for b in range(BLOCKS - 1):
+            rows = slice(b * P, (b + 1) * P)
+            quantize(nc, w1_rest_codes[:, rows], w1_rest_scales[:, rows], w1_rest_woven[:, rows, :])
+        rest_tops = keep.tile([P, BLOCKS - 1], F32, name="rest_tops")
+        rest_biases = keep.tile([P, BLOCKS - 1], F32, name="rest_biases")
+        for b in range(1, BLOCKS):
+            rows = slice((b - 1) * P, b * P)
             bank = psum.tile([P, H], F32, name="bank%d" % b)
-            product_into(bank[:], b, slice(0, H))
-            nc.vector.tensor_scalar(
-                h[b][:, 0:H], bank[:], 1.0, None, ALU.mult, ALU.max, accum_out=tops[:, b - 1 : b]
-            )
-            scale_bias.append((tau_sb[:, b, :], biases[:, b - 1 : b]))
-        nc.vector.scalar_tensor_tensor(biases[:], tops[:], -1.0, tau_sb[:, 1:, 0], ALU.mult, ALU.mult)
+            mx_product(nc, bank[:], w1_rest_codes[:, rows], w1_rest_scales[:, rows], z_codes[:], z_scales[:])
+            nc.vector.tensor_scalar(h[b], bank[:], 1.0, None, ALU.mult, ALU.max, accum_out=rest_tops[:, b - 1 : b])
+        nc.vector.scalar_tensor_tensor(rest_biases[:], rest_tops[:], -1.0, tau_sb[:, 1:, 0], ALU.mult, ALU.mult)
+        biases = [bias0[:]] + [rest_biases[:, b : b + 1] for b in range(BLOCKS - 1)]
 
-        pieces = []
-        f0 = 0
-        for wd in FIRST:
-            pieces.append((0, f0, wd, (f0, wd)))
-            f0 = f0 + wd
-        for b in range(1, N // P - 1):
-            pieces.extend([(b, 0, 256, None if MID else (0, 256)), (b, 256, 256, (0, 512) if MID else (256, 256))])
-        last = N // P - 1
-        f0 = 0
-        for wd in LAST:
-            pieces.append((last, f0, wd, (f0, wd)))
-            f0 = f0 + wd
+        mx = [keep.tile([P, H], F32, name="mx%d" % b) for b in range(BLOCKS)]
+        mn = [keep.tile([P, H], F32, name="mn%d" % b) for b in range(BLOCKS)]
+        spread = [keep.tile([P, H], F32, name="spread%d" % b) for b in range(BLOCKS)]
 
-        mx = [keep.tile([P, H], F32, name="mx%d" % b) for b in range(N // P)]
-        mn = [keep.tile([P, H], F32, name="mn%d" % b) for b in range(N // P)]
-        spread = [keep.tile([P, H], F32, name="spread%d" % b) for b in range(N // P)]
-
-        def finish_sub(b, cols):
-            nc.vector.tensor_tensor(spread[b][:, cols], mx[b][:, cols], mn[b][:, cols], ALU.subtract)
-
-        def finish_out(b, cols):
-            result = keep.tile([P, cols.stop - cols.start], F32, name="result_%d_%d" % (b, cols.start))
+        def finish(b, cols):
+            result = keep.tile([P, PIECE], F32, name="result_%d_%d" % (b, cols.start))
             nc.vector.scalar_tensor_tensor(result[:], spread[b][:, cols], 3.0, h[b][:, cols], ALU.mult, ALU.mult)
             nc.sync.dma_start(out[b * P : (b + 1) * P, cols], result[:])
 
-        previous = None
-        for b, first, width, stretch in pieces:
-            scale, bias = scale_bias[b]
-            name = "_%d_%d" % (b, first)
-            cols = slice(first, first + width)
-            ea = keep.tile([P, width, MEMBERS], F32, name="ea" + name)
-            flat = ea[:].rearrange("p j t -> p (j t)")
-            step = min(EXP_OFFSETS, width * MEMBERS)
-            for e0 in range(0, width * MEMBERS, step):
-                nc.scalar.activation(
-                    flat[:, e0 : e0 + step],
-                    h[b][:].indirect(entries(n4_sb, first * MEMBERS + e0, step)),
-                    ACT.Exp,
-                    bias=bias,
-                    scale=scale,
-                )
-            upper = keep.tile([P, width, 2], F32, name="upper" + name)
-            lower = keep.tile([P, width, 2], F32, name="lower" + name)
+        pieces = [(b, slice(first, first + PIECE)) for b in range(BLOCKS) for first in range(0, H, PIECE)]
+        for n, (b, cols) in enumerate(pieces):
+            ea = keep.tile([P, PIECE, MEMBERS], F32, name="ea%d" % n)
+            nc.scalar.activation(
+                ea[:].rearrange("p j t -> p (j t)"),
+                wide[b][:].indirect(entries(n4_sb, cols.start * MEMBERS, PIECE * MEMBERS)),
+                ACT.Exp,
+                bias=biases[b],
+                scale=tau_sb[:, b, :],
+            )
+            upper = keep.tile([P, PIECE, 2], F32, name="upper%d" % n)
+            lower = keep.tile([P, PIECE, 2], F32, name="lower%d" % n)
             nc.vector.tensor_tensor(upper[:], ea[:, :, 0:2], ea[:, :, 2:4], ALU.max)
             nc.vector.tensor_tensor(lower[:], ea[:, :, 0:2], ea[:, :, 2:4], ALU.min)
-            now = None if stretch is None else (b, slice(stretch[0], stretch[0] + stretch[1]))
-            if ORDER == 0:
-                if previous is not None:
-                    finish_sub(*previous)
-                nc.vector.tensor_tensor(mx[b][:, cols], upper[:, :, 0], upper[:, :, 1], ALU.max)
-                if previous is not None:
-                    finish_out(*previous)
-                nc.vector.tensor_tensor(mn[b][:, cols], lower[:, :, 0], lower[:, :, 1], ALU.min)
-            elif ORDER == 1:
-                nc.vector.tensor_tensor(mx[b][:, cols], upper[:, :, 0], upper[:, :, 1], ALU.max)
-                nc.vector.tensor_tensor(mn[b][:, cols], lower[:, :, 0], lower[:, :, 1], ALU.min)
-                if previous is not None:
-                    finish_out(*previous)
-                if now is not None:
-                    finish_sub(*now)
-            else:
-                nc.vector.tensor_tensor(mx[b][:, cols], upper[:, :, 0], upper[:, :, 1], ALU.max)
-                nc.vector.tensor_tensor(mn[b][:, cols], lower[:, :, 0], lower[:, :, 1], ALU.min)
-                if now is not None:
-                    finish_sub(*now)
-                    finish_out(*now)
-            previous = now
-        if ORDER == 0:
-            finish_sub(*previous)
-        if ORDER < 2:
-            finish_out(*previous)
+            nc.vector.tensor_tensor(mx[b][:, cols], upper[:, :, 0], upper[:, :, 1], ALU.max)
+            nc.vector.tensor_tensor(mn[b][:, cols], lower[:, :, 0], lower[:, :, 1], ALU.min)
+            if n > 0:
+                finish(*pieces[n - 1])
+            nc.vector.tensor_tensor(spread[b][:, cols], mx[b][:, cols], mn[b][:, cols], ALU.subtract)
+        finish(*pieces[-1])

from contextlib import ExitStack

import concourse.mybir as mybir

K, T, S, N, H, W = 512, 2048, 512, 512, 512, 2048
FLOPS = 2 * K * S * H + 2 * S * N * H

F32 = mybir.dt.float32
BF16 = mybir.dt.bfloat16
I32 = mybir.dt.int32
U32 = mybir.dt.uint32
U16 = mybir.dt.uint16
U8 = mybir.dt.uint8
FP8X4 = mybir.dt.float8_e4m3fn_x4
ALU = mybir.AluOpType
ACT = mybir.ActivationFunctionType

P = 128
PACK = 4
BLOCKS = N // P
LIST_ROWS = 16
MEMBERS = W // H
HALF = H // 2
Y_SPARE = 32
Z_PARTS = ((0, 256), (256, 128), (384, 128))
EARLY = Z_PARTS[-1][0]
PIECE = 256


def weave_views(woven, planes):
    return (
        woven.rearrange("p (c i) t -> p c t i", i=4),
        planes.rearrange("p t (c i) -> p c t i", i=4),
    )


def entries(offsets, first, count):
    return offsets[:, first // LIST_ROWS : (first + count) // LIST_ROWS]


def quantize(nc, codes, scales, woven):
    nc.vector.quantize_mx(out=codes.bitcast(FP8X4), scales=scales, in_=woven.rearrange("p n t -> p (n t)"))


def mx_product(nc, bank, lhs_codes, lhs_scales, rhs_codes, rhs_scales):
    nc.tensor.matmul_mx(
        out=bank,
        lhsT=lhs_codes.bitcast(FP8X4),
        lhsT_scale=lhs_scales,
        rhs=rhs_codes.bitcast(FP8X4),
        rhs_scale=rhs_scales,
        start=True,
        stop=True,
    )


def tile_picked_tokdotegp_none_p_kernel(
    tc, x_words, x_scales, wa, gt, w1, tau, offs, n1, n2, n3, n4, out
):
    nc = tc.nc
    with ExitStack() as ctx:
        lists = ctx.enter_context(tc.tile_pool(name="lists", bufs=1))
        keep = ctx.enter_context(tc.tile_pool(name="keep", bufs=1))
        psum = ctx.enter_context(tc.psum_pool(name="psum", bufs=1))

        offs_sb = lists.tile([P, S // LIST_ROWS], U16, name="offs_sb")
        n1_sb = lists.tile([P, H // LIST_ROWS], U16, name="n1_sb")
        n2_sb = lists.tile([P, H // LIST_ROWS], U16, name="n2_sb")
        n3_sb = lists.tile([P, H // LIST_ROWS], U16, name="n3_sb")
        n4_sb = lists.tile([P, W // LIST_ROWS], U16, name="n4_sb")

        wa_raw = [keep.tile([P, PACK, HALF], F32, name="wa_raw%d" % u) for u in range(2)]
        w1_first_raw = keep.tile([P, PACK, P], F32, name="w1_first_raw")
        w1_rest_raw = keep.tile([P, PACK, N - P], F32, name="w1_rest_raw")
        xw = keep.tile([P, T], I32, name="xw")
        xs = keep.tile([P, T], U8, name="xs")
        gt_sb = keep.tile([P, PACK], F32, name="gt_sb")
        tau_sb = keep.tile([P, BLOCKS, 1], F32, name="tau_sb")

        wa_rows = wa.rearrange("(p j) n -> p j n", j=PACK)
        w1_rows = w1.rearrange("(p j) n -> p j n", j=PACK)
        nc.vector.memset(xs[:, 0 : T // 2].bitcast(I32), 0)
        nc.gpsimd.memset(xs[:, T // 2 : T].bitcast(I32), 0)
        x_rows = x_words[0].rearrange("p n r -> p (n r)").bitcast(I32)
        nc.sync.dma_start(xw[:, 0 : T // 4], x_rows[:, 0 : T // 4])
        nc.sync.dma_start(offs_sb[:], offs)
        nc.sync.dma_start(xw[:, T // 4 : T // 2], x_rows[:, T // 4 : T // 2])
        for q in range(4):
            nc.sync.dma_start(
                xs[32 * q : 32 * q + 4, :].bitcast(I32), x_scales[0, 4 * q : 4 * q + 4, :].bitcast(I32)
            )
        nc.sync.dma_start(xw[:, T // 2 : T], x_rows[:, T // 2 : T])
        for u in range(2):
            nc.sync.dma_start(wa_raw[u][:], wa_rows[:, :, u * HALF : (u + 1) * HALF])
        nc.sync.dma_start(w1_first_raw[:], w1_rows[:, :, 0:P])
        nc.sync.dma_start(n3_sb[:], n3)
        nc.sync.dma_start(n1_sb[:], n1)
        nc.sync.dma_start(n2_sb[:], n2)
        nc.sync.dma_start(gt_sb[:], gt.rearrange("(p j) o -> p (j o)", j=PACK))
        nc.sync.dma_start(w1_rest_raw[:], w1_rows[:, :, P:N])
        nc.sync.dma_start(n4_sb[:], n4)
        with nc.allow_non_contiguous_dma(reason="one rate for each partition and row block"):
            nc.sync.dma_start(tau_sb[:], tau.rearrange("(b p) o -> p b o", p=P))

        xs_pick = keep.tile([P, S], U8, name="xs_pick", align_bytes=64)
        xw_pick = keep.tile([P, S], U32, name="xw_pick", align_bytes=64)
        nc.vector.tensor_copy(xs_pick[:].rearrange("p (t m) -> p m t", t=PACK), xs[:].indirect(offs_sb[:]))
        nc.vector.tensor_copy(
            xw_pick[:].rearrange("p (t m) -> p m t", t=PACK), xw[:].bitcast(U32).indirect(offs_sb[:])
        )

        wa_codes = keep.tile([P, H], U32, name="wa_codes", align_bytes=64)
        wa_scales = keep.tile([P, H], U8, name="wa_scales", align_bytes=64)
        wa_woven = [keep.tile([P, HALF, PACK], BF16, name="wa_woven%d" % u, align_bytes=64) for u in range(2)]
        nc.scalar.activation(*weave_views(wa_woven[0][:], wa_raw[0][:]), ACT.Copy)
        nc.vector.tensor_copy(*weave_views(wa_woven[1][:], wa_raw[1][:]))
        for u in range(2):
            cols = slice(u * HALF, (u + 1) * HALF)
            quantize(nc, wa_codes[:, cols], wa_scales[:, cols], wa_woven[u][:])

        w1_first_codes = keep.tile([P, P], U32, name="w1_first_codes", align_bytes=64)
        w1_rest_codes = keep.tile([P, N - P], U32, name="w1_rest_codes", align_bytes=64)
        w1_first_scales = keep.tile([P, P], U8, name="w1_first_scales", align_bytes=64)
        w1_first_woven = keep.tile([P, P, PACK], BF16, name="w1_first_woven", align_bytes=64)
        nc.scalar.activation(*weave_views(w1_first_woven[:], w1_first_raw[:]), ACT.Copy)

        def first_product(bank, t, cols):
            tokens = slice(t * P, (t + 1) * P)
            mx_product(nc, bank, xw_pick[:, tokens], xs_pick[:, tokens], wa_codes[:, cols], wa_scales[:, cols])

        y = [keep.tile([P, H + Y_SPARE], F32, name="y%d" % t) for t in range(PACK)]
        y0_low = psum.tile([P, HALF], F32, name="y0_low")
        y0_high = psum.tile([P, HALF], F32, name="y0_high")
        first_product(y0_low[:], 0, slice(0, HALF))
        first_product(y0_high[:], 0, slice(HALF, H))
        nc.scalar.activation(y[0][:, 0:HALF], y0_low[:], ACT.Copy)
        nc.vector.tensor_copy(y[0][:, HALF:H], y0_high[:])
        for t in range(1, PACK):
            bank = psum.tile([P, H], F32, name="bank%d" % t)
            first_product(bank[:], t, slice(0, H))
            if t == PACK - 1:
                gain = keep.tile([P, PACK], F32, name="gain", tag="wa_scales", align_bytes=64)
                nc.vector.tensor_scalar(gain[:], gt_sb[:], 0.75, None, ALU.mult)
            nc.vector.tensor_copy(y[t][:, 0:H], bank[:])

        wide = [keep.tile([P, 4 * H], F32, name="wide%d" % n) for n in range(BLOCKS)]
        z_codes = keep.tile([P, H], U32, name="z_codes", align_bytes=64)
        z_scales = keep.tile([P, H], U8, name="z_scales", align_bytes=64)
        z_planes = keep.tile([P, PACK, H], BF16, name="z_planes", align_bytes=64)
        z_woven = [keep.tile([P, n, PACK], BF16, name="z_woven%d" % f, align_bytes=64) for f, n in Z_PARTS]
        cross = keep.tile([P, PACK * H], F32, name="cross", tag="wa_codes", align_bytes=64)

        def look_up(dst, t, offsets, first, width):
            nc.scalar.activation(dst, y[t][:].indirect(entries(offsets, first, width)), ACT.Copy)

        def plane(t, n, first, width):
            return wide[t][:, n * H + first : n * H + first + width]

        def cross_of(t, first, width):
            return cross[:, t * H + first : t * H + first + width]

        def make_cross(t, first, width):
            look_up(plane(t, 2, first, width), t, n3_sb, first, width)
            look_up(plane(t, 3, first, width), t, n1_sb, first, width)
            nc.vector.tensor_tensor(
                cross_of(t, first, width),
                y[t][:].indirect(entries(n2_sb, first, width)),
                plane(t, 2, first, width),
                ALU.mult,
            )

        def make_own(t, first, width):
            nc.vector.scalar_tensor_tensor(
                plane(t, 1, first, width),
                plane(t, 3, first, width),
                gain[:, t : t + 1],
                y[t][:, first : first + width],
                ALU.mult,
                ALU.mult,
            )

        def make_z(t, first, width):
            nc.vector.scalar_tensor_tensor(
                z_planes[:, t, first : first + width],
                cross_of(t, first, width),
                gain[:, t : t + 1],
                plane(t, 1, first, width),
                ALU.mult,
                ALU.add,
            )

        def weave_z(part):
            first, width = Z_PARTS[part]
            views = weave_views(z_woven[part][:], z_planes[:, :, first : first + width])
            if part == 0:
                nc.scalar.copy(*views)
            else:
                nc.vector.tensor_copy(*views)

        def quantize_z(part):
            first, width = Z_PARTS[part]
            cols = slice(first, first + width)
            quantize(nc, z_codes[:, cols], z_scales[:, cols], z_woven[part][:])

        steps = [(t, 0, H) for t in range(PACK - 1)] + [(PACK - 1, first, width) for first, width in Z_PARTS]
        for n, step in enumerate(steps):
            make_cross(*step)
            if n > 0:
                make_z(*steps[n - 1])
            make_own(*step)
            if n == 0:
                quantize(nc, w1_first_codes[:], w1_first_scales[:], w1_first_woven[:])
            done = n - PACK
            if done > 0:
                quantize_z(done - 1)
            if done >= 0:
                weave_z(done)
        last = len(Z_PARTS) - 1
        make_z(*steps[-1])
        quantize_z(last - 1)
        weave_z(last)
        quantize_z(last)

        h = [wide[b][:, 0:H] for b in range(BLOCKS)]
        top0 = keep.tile([P, 1], F32, name="top0", align_bytes=64)
        bias0 = keep.tile([P, 1], F32, name="bias0")
        early = psum.tile([P, EARLY], F32, name="h0_early")
        late = psum.tile([P, H - EARLY], F32, name="h0_late")
        early_top = keep.tile([P, 1], F32, name="early_top")
        for first, width in Z_PARTS:
            cols = slice(first, first + width)
            bank_cols = early[:, cols] if first < EARLY else late[:]
            mx_product(nc, bank_cols, w1_first_codes[:], w1_first_scales[:], z_codes[:, cols], z_scales[:, cols])
        nc.vector.tensor_scalar(h[0][:, 0:EARLY], early[:], 1.0, None, ALU.mult, ALU.max, accum_out=early_top[:])
        nc.vector.tensor_scalar(h[0][:, EARLY:H], late[:], 1.0, early_top[:], ALU.mult, ALU.max, accum_out=top0[:])
        nc.vector.tensor_scalar(bias0[:], top0[:], tau_sb[:, 0, :], -1.0, ALU.mult, ALU.mult)

        w1_rest_woven = keep.tile([P, N - P, PACK], BF16, name="w1_rest_woven", tag="wa_codes", align_bytes=64)
        w1_rest_scales = keep.tile([P, N - P], U8, name="w1_rest_scales", tag="top0", align_bytes=64)
        nc.scalar.activation(*weave_views(w1_rest_woven[:], w1_rest_raw[:]), ACT.Copy)
        for b in range(BLOCKS - 1):
            rows = slice(b * P, (b + 1) * P)
            quantize(nc, w1_rest_codes[:, rows], w1_rest_scales[:, rows], w1_rest_woven[:, rows, :])
        rest_tops = keep.tile([P, BLOCKS - 1], F32, name="rest_tops")
        rest_biases = keep.tile([P, BLOCKS - 1], F32, name="rest_biases")
        for b in range(1, BLOCKS):
            rows = slice((b - 1) * P, b * P)
            bank = psum.tile([P, H], F32, name="bank%d" % b)
            mx_product(nc, bank[:], w1_rest_codes[:, rows], w1_rest_scales[:, rows], z_codes[:], z_scales[:])
            nc.vector.tensor_scalar(h[b], bank[:], 1.0, None, ALU.mult, ALU.max, accum_out=rest_tops[:, b - 1 : b])
        nc.vector.scalar_tensor_tensor(rest_biases[:], rest_tops[:], -1.0, tau_sb[:, 1:, 0], ALU.mult, ALU.mult)
        biases = [bias0[:]] + [rest_biases[:, b : b + 1] for b in range(BLOCKS - 1)]

        mx = [keep.tile([P, H], F32, name="mx%d" % b) for b in range(BLOCKS)]
        mn = [keep.tile([P, H], F32, name="mn%d" % b) for b in range(BLOCKS)]
        spread = [keep.tile([P, H], F32, name="spread%d" % b) for b in range(BLOCKS)]

        def finish(b, cols):
            result = keep.tile([P, PIECE], F32, name="result_%d_%d" % (b, cols.start))
            nc.vector.scalar_tensor_tensor(result[:], spread[b][:, cols], 3.0, h[b][:, cols], ALU.mult, ALU.mult)
            nc.sync.dma_start(out[b * P : (b + 1) * P, cols], result[:])

        pieces = [(b, slice(first, first + PIECE)) for b in range(BLOCKS) for first in range(0, H, PIECE)]
        for n, (b, cols) in enumerate(pieces):
            ea = keep.tile([P, PIECE, MEMBERS], F32, name="ea%d" % n)
            nc.scalar.activation(
                ea[:].rearrange("p j t -> p (j t)"),
                wide[b][:].indirect(entries(n4_sb, cols.start * MEMBERS, PIECE * MEMBERS)),
                ACT.Exp,
                bias=biases[b],
                scale=tau_sb[:, b, :],
            )
            upper = keep.tile([P, PIECE, 2], F32, name="upper%d" % n)
            lower = keep.tile([P, PIECE, 2], F32, name="lower%d" % n)
            nc.vector.tensor_tensor(upper[:], ea[:, :, 0:2], ea[:, :, 2:4], ALU.max)
            nc.vector.tensor_tensor(lower[:], ea[:, :, 0:2], ea[:, :, 2:4], ALU.min)
            nc.vector.tensor_tensor(mx[b][:, cols], upper[:, :, 0], upper[:, :, 1], ALU.max)
            nc.vector.tensor_tensor(mn[b][:, cols], lower[:, :, 0], lower[:, :, 1], ALU.min)
            if n > 0:
                finish(*pieces[n - 1])
            nc.vector.tensor_tensor(spread[b][:, cols], mx[b][:, cols], mn[b][:, cols], ALU.subtract)
        finish(*pieces[-1])
